import numpy as np
import ml_dtypes


def mxq(x, axis, fmt="e4m3"):
    dtype, down = {"e4m3": (ml_dtypes.float8_e4m3fn, 7), "e5m2": (ml_dtypes.float8_e5m2, 14)}[fmt]
    v = np.moveaxis(np.asarray(x, np.float32).astype(ml_dtypes.bfloat16).astype(np.float64), axis, -1)
    blocks = v.reshape(v.shape[:-1] + (-1, 32))
    amax = np.abs(blocks).max(-1, keepdims=True)
    byte = np.maximum(np.where(amax > 0, np.frexp(amax)[1] - 1 + 127, 0) - down, 1)
    scale = np.exp2(byte - 127.0)
    codes = (blocks / scale).astype(np.float32).astype(dtype).astype(np.float64)
    return np.moveaxis((codes * scale).reshape(v.shape), -1, axis)


WIDE = False


def mx_kscale(k):
    if not WIDE:
        return np.ones(k)
    levels = np.array([10, -10, 5, -5, 0])
    if k % 512:
        return np.exp2(np.random.permutation(np.resize(levels, k // 32))).repeat(32)
    a = np.empty((k // 512, 16))
    for p in range(k // 512):
        a[p, :8] = np.random.permutation(np.resize(levels, 8))
        for g in range(8):
            far = levels[np.abs(levels - a[p, g]) >= 10]
            a[p, g + 8] = far[np.random.randint(len(far))]
    return np.exp2(a.ravel()).repeat(32)


def f64(x):
    return np.asarray(x).astype(np.float64)


def striped(idx):
    return np.tile(np.asarray(idx).reshape(-1, 16).T, (8, 1)).astype(np.uint16)


def unstriped(offs):
    return offs[:16].T.reshape(-1).astype(np.int64)


E2M1 = np.array([0.0, 0.5, 1.0, 1.5, 2.0, 3.0, 4.0, 6.0, -0.0, -0.5, -1.0, -1.5, -2.0, -3.0, -4.0, -6.0])


def pack_weight(w, fmt):
    k, n = w.shape
    w = f64(np.asarray(w, np.float32).astype(ml_dtypes.bfloat16)).reshape(k // 32, 32, n)
    amax = np.abs(w).max(1)
    if fmt == "e4m3":
        byte = np.frexp(amax)[1] - 1 + 127 - 7
    else:
        mant, ex = np.frexp(amax / 6.0)
        byte = np.where(mant > 0.5, ex, ex - 1) + 127
    byte = np.clip(np.where(amax > 0, byte, 1), 1, 254)
    scaled = (w * np.exp2(127.0 - byte)[:, None, :]).reshape(k, n).astype(np.float32)
    by_word = np.ascontiguousarray(scaled.reshape(k // 512, 128, 4, n).transpose(0, 1, 3, 2))
    if fmt == "e4m3":
        words = by_word.astype(ml_dtypes.float8_e4m3fn).view(np.uint8)
    else:
        c = by_word.astype(ml_dtypes.float4_e2m1fn).view(np.uint8) & 0xF
        words = (c[..., 0::2] | (c[..., 1::2] << 4)).reshape(k // 512, 128, 2 * n)
    return np.ascontiguousarray(words), np.ascontiguousarray(byte.astype(np.uint8).reshape(k // 512, 16, n))


def unpack_weight(words, scales, fmt):
    g, _, n = scales.shape
    words = np.ascontiguousarray(words).reshape(g, 128, n, -1)
    if fmt == "e4m3":
        vals = words.view(ml_dtypes.float8_e4m3fn).astype(np.float64)
    else:
        nib = np.empty((g, 128, n, 4), np.uint8)
        nib[..., 0::2] = words & 0xF
        nib[..., 1::2] = words >> 4
        vals = E2M1[nib]
    vals = vals * np.repeat(np.exp2(scales.astype(np.float64) - 127.0), 8, axis=1)[..., None]
    return vals.transpose(0, 1, 3, 2).reshape(g * 512, n)


B, N, T, D, DV, NQ = 1, 512, 1024, 512, 256, 256


def setup_inputs():
    n = np.random.standard_normal
    idx = np.random.permutation(T)[:B * N]
    s = mx_kscale(D)[:, None]
    u = np.ones(T)
    u[idx] = mx_kscale(B * N)
    r = np.random.uniform(0.5, 2.0, T)
    qp = [pack_weight(x, "e4m3") for x in n((B, D, NQ)) * s * (0.80 / np.sqrt(D))]
    k = n((D, T)) / s
    v = n((DV, T)) / (u * r)
    kp = pack_weight(k, "e4m3")
    return {
        "q_words": np.stack([x[0] for x in qp]),
        "q_scales": np.stack([x[1] for x in qp]),
        "k_words": kp[0],
        "k_scales": kp[1],
        "vT": v.astype(np.float32),
        "vs": np.tile(u * r, (128, 1)).astype(np.float32),
        "offs": striped(idx),
    }


def reference(q_words, q_scales, k_words, k_scales, vT, vs, offs):
    idx = unstriped(offs)
    k = unpack_weight(k_words, k_scales, "e4m3")
    v = f64(vT)
    pick = lambda x: x[:, idx].reshape(x.shape[0], B, N).transpose(1, 0, 2)
    q = np.stack([unpack_weight(q_words[b], q_scales[b], "e4m3") for b in range(B)])
    score = q.transpose(0, 2, 1) @ pick(k)
    m = score.max(-1, keepdims=True)
    p = np.exp(score - m)
    total = p.sum(-1, keepdims=True)
    w = p * pick(f64(vs))[:, :1, :]
    y = mxq(w, 2, "e4m3") @ mxq(pick(v).transpose(0, 2, 1), 1, "e4m3")
    y = y / total
    return y

@@ -1,0 +1,146 @@
+from contextlib import ExitStack
+
+import concourse.mybir as mybir
+from concourse.masks import make_identity
+
+F32 = mybir.dt.float32
+BF16 = mybir.dt.bfloat16
+I32 = mybir.dt.int32
+U32 = mybir.dt.uint32
+U16 = mybir.dt.uint16
+U8 = mybir.dt.uint8
+FP8X4 = mybir.dt.float8_e4m3fn_x4
+ACT = mybir.ActivationFunctionType
+ALU = mybir.AluOpType
+AXIS = mybir.AxisListType
+
+P = 128
+PACK = 4
+N, T, D, DV, NQ = 512, 1024, 512, 256, 256
+FLOPS = 2 * NQ * N * D + 2 * NQ * N * DV
+BYTES = 4 * P * NQ + 16 * NQ + 4 * P * T + 16 * T + 4 * DV * T + 4 * T + 2 * P * (N // 16) + 4 * NQ * DV
+
+
+def tile_attend_qpk_topk_kernel(tc, q_words, q_scales, k_words, k_scales, vT, vs, offs, out):
+    nc = tc.nc
+    with ExitStack() as ctx:
+        sb = ctx.enter_context(tc.tile_pool(name="sb", bufs=1))
+        ps = ctx.enter_context(tc.psum_pool(name="ps", bufs=1))
+
+        offsets = sb.tile([P, N // 16], U16, name="offsets")
+        k_pool = sb.tile([P, T], U32, name="k_pool", align_bytes=64)
+        ks_pool = sb.tile([P, T], U8, name="ks_pool", align_bytes=64)
+        q_codes = sb.tile([P, NQ], U32, name="q_codes", align_bytes=64)
+        q_plane = sb.tile([P, NQ], U8, name="q_plane", align_bytes=64)
+        vs_pool = sb.tile([P, T], F32, name="vs_pool", align_bytes=64)
+        v_pool = [sb.tile([P, T], F32, name=f"v_pool{h}", align_bytes=64) for h in range(2)]
+        ident = sb.tile([P, P], F32, name="ident", align_bytes=64)
+        warm = sb.tile([P, 1], F32, name="warm")
+        warm_out = sb.tile([P, 1], F32, name="warm_out")
+
+        nc.vector.memset(ks_pool[:].bitcast(I32), 0)
+        nc.vector.memset(q_plane[:].bitcast(I32), 0)
+        nc.vector.memset(warm[:], 0.0)
+        nc.gpsimd.memset(vs_pool[:], 0.0)
+        make_identity(nc, ident[:])
+
+        nc.sync.dma_start(offsets[:], offs)
+        for quad in range(4):
+            eng = nc.sync if quad < 2 else nc.scalar
+            eng.dma_start(ks_pool[32 * quad : 32 * quad + 4, :].bitcast(I32), k_scales[0, 4 * quad : 4 * quad + 4, :].bitcast(I32))
+        nc.sync.dma_start(k_pool[:].bitcast(I32), k_words[0].rearrange("p t r -> p (t r)").bitcast(I32))
+        nc.sync.dma_start(q_codes[:].bitcast(I32), q_words[0, 0].rearrange("p t r -> p (t r)").bitcast(I32))
+        nc.sync.dma_start(v_pool[1][:], vT[P : 2 * P, :])
+        nc.scalar.activation(warm_out[:], warm[:], ACT.Exp)
+        for quad in range(4):
+            nc.sync.dma_start(q_plane[32 * quad : 32 * quad + 4, :].bitcast(I32), q_scales[0, 0, 4 * quad : 4 * quad + 4, :].bitcast(I32))
+        nc.sync.dma_start(vs_pool[0:1, :], vs[0:1, :])
+        nc.sync.dma_start(v_pool[0][:], vT[0:P, :])
+
+        ks_g = sb.tile([P, N], U8, name="ks_g", align_bytes=64)
+        k_g = sb.tile([P, N], U32, name="k_g", align_bytes=64)
+        vs_g = sb.tile([P, N], F32, name="vs_g", align_bytes=64)
+        nc.vector.tensor_copy(ks_g[:], ks_pool[:].indirect(offsets[:]))
+        nc.vector.tensor_copy(k_g[:], k_pool[:].indirect(offsets[:]))
+
+        score = [ps.tile([P, N], F32, name=f"score{i}", tag=f"acc{i}") for i in range(2)]
+        for i in range(2):
+            cols = slice(i * P, (i + 1) * P)
+            nc.tensor.matmul_mx(out=score[i][:], lhsT=q_codes[:, cols].bitcast(FP8X4), lhsT_scale=q_plane[:, cols],
+                                rhs=k_g[:].bitcast(FP8X4), rhs_scale=ks_g[:], start=True, stop=True)
+
+        nc.vector.tensor_copy(vs_g[:], vs_pool[:].indirect(offsets[:]))
+        vs_turn = ps.tile([P, PACK, P], F32, name="vs_turn")
+        for t in range(PACK):
+            nc.tensor.transpose(vs_turn[:, t, :], vs_g[:, t:N:PACK], ident[:])
+        vs_col = sb.tile([P, 1, PACK], F32, name="vs_col")
+
+        v_g = [sb.tile([P, N], BF16, name=f"v_g{h}", align_bytes=64) for h in range(2)]
+        v_bf = sb.tile([P, T], BF16, name="v_bf", align_bytes=64)
+        nc.scalar.copy(v_bf[:], v_pool[1][:])
+        nc.scalar.activation(v_g[1][:], v_bf[:].indirect(offsets[:]), ACT.Copy)
+
+        neg_max = [sb.tile([P, 1], F32, name=f"neg_max{i}") for i in range(2)]
+        total = sb.tile([P, 2], F32, name="total")
+        prob = [sb.tile([P, PACK, P], F32, name=f"prob{i}", align_bytes=64) for i in range(2)]
+        for i in range(2):
+            nc.vector.tensor_reduce(neg_max[i][:], score[i][:], AXIS.X, ALU.max, negate=True)
+        for i in range(2):
+            nc.scalar.activation(prob[i][:], score[i][:].rearrange("p (s t) -> p t s", t=PACK), ACT.Exp,
+                                 bias=neg_max[i][:], scale=1.0, accum_out=total[:, i : i + 1])
+        nc.scalar.copy(vs_col[:, 0, :], vs_turn[:, :, 0])
+        nc.vector.tensor_copy(v_g[0][:], v_pool[0][:].indirect(offsets[:]))
+
+        v_in = sb.tile([P, DV, PACK], BF16, name="v_in", align_bytes=64)
+        v_turn = [ps.tile([P, 2, P], F32, name=f"v_turn{h}") for h in range(2)]
+        p_turn = [ps.tile([P, PACK, P], F32, name=f"p_turn{i}") for i in range(2)]
+
+        def turn_values(h):
+            words = v_g[h][:].bitcast(F32)
+            for u in range(2):
+                nc.tensor.transpose(v_turn[h][:, u, :], words[:, u : N // 2 : 2], ident[:])
+            dst = v_in[:, h * P : (h + 1) * P, :].rearrange("p e t -> p (e t)").bitcast(F32)
+            nc.scalar.copy(dst.rearrange("p (e u) -> p e u", u=2), v_turn[h][:].rearrange("p u e -> p e u"))
+
+        def turn_weights(i):
+            for t in range(PACK):
+                nc.tensor.transpose(p_turn[i][:, t, :], prob[i][:, t, :], ident[:])
+
+        turn_values(1)
+        turn_weights(0)
+        turn_weights(1)
+        turn_values(0)
+
+        w_in = [sb.tile([P, P, PACK], BF16, name=f"w_in{i}", align_bytes=64) for i in range(2)]
+        w_codes = [sb.tile([P, P], U32, name=f"w_codes{i}", align_bytes=64) for i in range(2)]
+        w_plane = [sb.tile([P, P], U8, name=f"w_plane{i}", align_bytes=64) for i in range(2)]
+        v_codes = sb.tile([P, DV], U32, name="v_codes", align_bytes=64)
+        v_plane = sb.tile([P, DV], U8, name="v_plane", align_bytes=64)
+        inv = sb.tile([P, 2], F32, name="inv")
+
+        def weigh(i):
+            nc.vector.tensor_tensor(w_in[i][:], p_turn[i][:].rearrange("p t q -> p q t"),
+                                    vs_col[:].to_broadcast([P, P, PACK]), ALU.mult)
+
+        def quantise_w(i):
+            nc.vector.quantize_mx(out=w_codes[i][:].bitcast(FP8X4), scales=w_plane[i][:],
+                                  in_=w_in[i][:].rearrange("p q t -> p (q t)"))
+
+        weigh(0)
+        nc.vector.reciprocal(inv[:], total[:])
+        nc.vector.quantize_mx(out=v_codes[:].bitcast(FP8X4), scales=v_plane[:], in_=v_in[:].rearrange("p e t -> p (e t)"))
+        weigh(1)
+        quantise_w(0)
+        quantise_w(1)
+
+        for i in range(2):
+            y = ps.tile([P, DV], F32, name=f"y{i}", tag=f"acc{i}")
+            nc.tensor.matmul_mx(out=y[:], lhsT=w_codes[i][:].bitcast(FP8X4), lhsT_scale=w_plane[i][:],
+                                rhs=v_codes[:].bitcast(FP8X4), rhs_scale=v_plane[:], start=True, stop=True)
+            res = sb.tile([P, DV], F32, name=f"res{i}", align_bytes=64)
+            if i == 0:
+                nc.scalar.activation(res[:], y[:], ACT.Copy, scale=inv[:, i : i + 1])
+                nc.scalar.dma_start(out[0, i * P : (i + 1) * P, :], res[:])
+            else:
+                nc.vector.tensor_scalar(res[:], y[:], inv[:, i : i + 1], None, ALU.mult)
+                nc.sync.dma_start(out[0, i * P : (i + 1) * P, :], res[:])

@@ -25,43 +25,45 @@ def tile_attend_qpk_topk_kernel(tc, q_words, q_scales, k_words, k_scales, vT, vs
     nc = tc.nc
     with ExitStack() as ctx:
         sb = ctx.enter_context(tc.tile_pool(name="sb", bufs=1))
+        lap = ctx.enter_context(tc.tile_pool(name="lap", bufs=1))
         ps = ctx.enter_context(tc.psum_pool(name="ps", bufs=1))
 
         offsets = sb.tile([P, N // 16], U16, name="offsets")
-        k_pool = sb.tile([P, T], U32, name="k_pool", align_bytes=64)
+        k_pool = sb.tile([P, T], U32, name="k_pool", tag="late", align_bytes=64)
         ks_pool = sb.tile([P, T], U8, name="ks_pool", align_bytes=64)
-        q_codes = sb.tile([P, NQ], U32, name="q_codes", align_bytes=64)
+        vs_pool = lap.tile([P, T], F32, name="vs_pool", offset=0, align_bytes=64)
         q_plane = sb.tile([P, NQ], U8, name="q_plane", align_bytes=64)
-        vs_pool = sb.tile([P, T], F32, name="vs_pool", align_bytes=64)
-        v_pool = [sb.tile([P, T], F32, name=f"v_pool{h}", align_bytes=64) for h in range(2)]
         ident = sb.tile([P, P], F32, name="ident", align_bytes=64)
-        warm = sb.tile([P, 1], F32, name="warm")
-        warm_out = sb.tile([P, 1], F32, name="warm_out")
+        warm_in = sb.tile([P, 1], F32, name="warm_in", tag="v_hi", align_bytes=64)
+        warm_out = sb.tile([P, 1], F32, name="warm_out", tag="q_codes", align_bytes=64)
 
         nc.vector.memset(ks_pool[:].bitcast(I32), 0)
+        nc.vector.memset(warm_in[:], 0.0)
+        nc.vector.memset(vs_pool[:, : T - P].bitcast(I32), 0)
         nc.vector.memset(q_plane[:].bitcast(I32), 0)
-        nc.vector.memset(warm[:], 0.0)
-        nc.gpsimd.memset(vs_pool[:], 0.0)
+        nc.vector.memset(vs_pool[:, T - P :].bitcast(I32), 0)
         make_identity(nc, ident[:])
+        nc.scalar.activation(warm_out[:], warm_in[:], ACT.Exp)
 
         nc.sync.dma_start(offsets[:], offs)
-        for quad in range(4):
-            eng = nc.sync if quad < 2 else nc.scalar
-            eng.dma_start(ks_pool[32 * quad : 32 * quad + 4, :].bitcast(I32), k_scales[0, 4 * quad : 4 * quad + 4, :].bitcast(I32))
         nc.sync.dma_start(k_pool[:].bitcast(I32), k_words[0].rearrange("p t r -> p (t r)").bitcast(I32))
+        for quad in range(4):
+            nc.sync.dma_start(ks_pool[32 * quad : 32 * quad + 4, :].bitcast(I32), k_scales[0, 4 * quad : 4 * quad + 4, :].bitcast(I32))
+        v_hi = sb.tile([P, T], F32, name="v_hi", tag="v_hi", align_bytes=64)
+        q_codes = sb.tile([P, NQ], U32, name="q_codes", tag="q_codes", align_bytes=64)
+        nc.sync.dma_start(v_hi[:], vT[P : 2 * P, :])
         nc.sync.dma_start(q_codes[:].bitcast(I32), q_words[0, 0].rearrange("p t r -> p (t r)").bitcast(I32))
-        nc.sync.dma_start(v_pool[1][:], vT[P : 2 * P, :])
-        nc.scalar.activation(warm_out[:], warm[:], ACT.Exp)
         for quad in range(4):
             nc.sync.dma_start(q_plane[32 * quad : 32 * quad + 4, :].bitcast(I32), q_scales[0, 0, 4 * quad : 4 * quad + 4, :].bitcast(I32))
         nc.sync.dma_start(vs_pool[0:1, :], vs[0:1, :])
-        nc.sync.dma_start(v_pool[0][:], vT[0:P, :])
 
         ks_g = sb.tile([P, N], U8, name="ks_g", align_bytes=64)
-        k_g = sb.tile([P, N], U32, name="k_g", align_bytes=64)
+        k_g = lap.tile([P, N], U32, name="k_g", offset=4096, align_bytes=64)
         vs_g = sb.tile([P, N], F32, name="vs_g", align_bytes=64)
-        nc.vector.tensor_copy(ks_g[:], ks_pool[:].indirect(offsets[:]))
         nc.vector.tensor_copy(k_g[:], k_pool[:].indirect(offsets[:]))
+        nc.vector.tensor_copy(ks_g[:], ks_pool[:].indirect(offsets[:]))
+        v_lo = sb.tile([P, T], F32, name="v_lo", tag="late", align_bytes=64)
+        nc.sync.dma_start(v_lo[:], vT[0:P, :])
 
         score = [ps.tile([P, N], F32, name=f"score{i}", tag=f"acc{i}") for i in range(2)]
         for i in range(2):
@@ -70,17 +72,16 @@ def tile_attend_qpk_topk_kernel(tc, q_words, q_scales, k_words, k_scales, vT, vs
                                 rhs=k_g[:].bitcast(FP8X4), rhs_scale=ks_g[:], start=True, stop=True)
 
         nc.vector.tensor_copy(vs_g[:], vs_pool[:].indirect(offsets[:]))
-        vs_turn = ps.tile([P, PACK, P], F32, name="vs_turn")
+        vs_turn = ps.tile([P, PACK, P], F32, name="vs_turn", tag="vs_turn")
         for t in range(PACK):
             nc.tensor.transpose(vs_turn[:, t, :], vs_g[:, t:N:PACK], ident[:])
-        vs_col = sb.tile([P, 1, PACK], F32, name="vs_col")
 
-        v_g = [sb.tile([P, N], BF16, name=f"v_g{h}", align_bytes=64) for h in range(2)]
+        v_g = [lap.tile([P, N], BF16, name=f"v_g{h}", offset=(3584, 6144)[h], align_bytes=64) for h in range(2)]
         v_bf = sb.tile([P, T], BF16, name="v_bf", align_bytes=64)
-        nc.scalar.copy(v_bf[:], v_pool[1][:])
+        nc.scalar.copy(v_bf[:], v_hi[:])
         nc.scalar.activation(v_g[1][:], v_bf[:].indirect(offsets[:]), ACT.Copy)
 
-        neg_max = [sb.tile([P, 1], F32, name=f"neg_max{i}") for i in range(2)]
+        neg_max = [lap.tile([P, 1], F32, name=f"neg_max{i}", offset=64 * i, align_bytes=64) for i in range(2)]
         total = sb.tile([P, 2], F32, name="total")
         prob = [sb.tile([P, PACK, P], F32, name=f"prob{i}", align_bytes=64) for i in range(2)]
         for i in range(2):
@@ -88,11 +89,12 @@ def tile_attend_qpk_topk_kernel(tc, q_words, q_scales, k_words, k_scales, vT, vs
         for i in range(2):
             nc.scalar.activation(prob[i][:], score[i][:].rearrange("p (s t) -> p t s", t=PACK), ACT.Exp,
                                  bias=neg_max[i][:], scale=1.0, accum_out=total[:, i : i + 1])
+        vs_col = lap.tile([P, 1, PACK], F32, name="vs_col", offset=0, align_bytes=64)
         nc.scalar.copy(vs_col[:, 0, :], vs_turn[:, :, 0])
-        nc.vector.tensor_copy(v_g[0][:], v_pool[0][:].indirect(offsets[:]))
+        nc.vector.tensor_copy(v_g[0][:], v_lo[:].indirect(offsets[:]))
 
-        v_in = sb.tile([P, DV, PACK], BF16, name="v_in", align_bytes=64)
-        v_turn = [ps.tile([P, 2, P], F32, name=f"v_turn{h}") for h in range(2)]
+        v_in = lap.tile([P, DV, PACK], BF16, name="v_in", offset=64, align_bytes=64)
+        v_turn = [ps.tile([P, 2, P], F32, name=f"v_turn{h}", tag=("acc1", "vs_turn")[h]) for h in range(2)]
         p_turn = [ps.tile([P, PACK, P], F32, name=f"p_turn{i}") for i in range(2)]
 
         def turn_values(h):
@@ -106,9 +108,9 @@ def tile_attend_qpk_topk_kernel(tc, q_words, q_scales, k_words, k_scales, vT, vs
             for t in range(PACK):
                 nc.tensor.transpose(p_turn[i][:, t, :], prob[i][:, t, :], ident[:])
 
-        turn_values(1)
         turn_weights(0)
         turn_weights(1)
+        turn_values(1)
         turn_values(0)
 
         w_in = [sb.tile([P, P, PACK], BF16, name=f"w_in{i}", align_bytes=64) for i in range(2)]
@@ -116,7 +118,7 @@ def tile_attend_qpk_topk_kernel(tc, q_words, q_scales, k_words, k_scales, vT, vs
         w_plane = [sb.tile([P, P], U8, name=f"w_plane{i}", align_bytes=64) for i in range(2)]
         v_codes = sb.tile([P, DV], U32, name="v_codes", align_bytes=64)
         v_plane = sb.tile([P, DV], U8, name="v_plane", align_bytes=64)
-        inv = sb.tile([P, 2], F32, name="inv")
+        inv = lap.tile([P, 2], F32, name="inv", offset=0, align_bytes=64)
 
         def weigh(i):
             nc.vector.tensor_tensor(w_in[i][:], p_turn[i][:].rearrange("p t q -> p q t"),
@@ -127,14 +129,14 @@ def tile_attend_qpk_topk_kernel(tc, q_words, q_scales, k_words, k_scales, vT, vs
                                   in_=w_in[i][:].rearrange("p q t -> p (q t)"))
 
         weigh(0)
-        nc.vector.reciprocal(inv[:], total[:])
-        nc.vector.quantize_mx(out=v_codes[:].bitcast(FP8X4), scales=v_plane[:], in_=v_in[:].rearrange("p e t -> p (e t)"))
         weigh(1)
         quantise_w(0)
+        nc.vector.quantize_mx(out=v_codes[:].bitcast(FP8X4), scales=v_plane[:], in_=v_in[:].rearrange("p e t -> p (e t)"))
         quantise_w(1)
+        nc.vector.reciprocal(inv[:], total[:])
 
         for i in range(2):
-            y = ps.tile([P, DV], F32, name=f"y{i}", tag=f"acc{i}")
+            y = ps.tile([P, DV], F32, name=f"y{i}", tag=("acc0", "y1")[i])
             nc.tensor.matmul_mx(out=y[:], lhsT=w_codes[i][:].bitcast(FP8X4), lhsT_scale=w_plane[i][:],
                                 rhs=v_codes[:].bitcast(FP8X4), rhs_scale=v_plane[:], start=True, stop=True)
             res = sb.tile([P, DV], F32, name=f"res{i}", align_bytes=64)

@@ -45,8 +45,8 @@ def tile_attend_qpk_topk_kernel(tc, q_words, q_scales, k_words, k_scales, vT, vs
         make_identity(nc, ident[:])
         nc.scalar.activation(warm_out[:], warm_in[:], ACT.Exp)
 
-        nc.sync.dma_start(offsets[:], offs)
         nc.sync.dma_start(k_pool[:].bitcast(I32), k_words[0].rearrange("p t r -> p (t r)").bitcast(I32))
+        nc.sync.dma_start(offsets[:], offs)
         for quad in range(4):
             nc.sync.dma_start(ks_pool[32 * quad : 32 * quad + 4, :].bitcast(I32), k_scales[0, 4 * quad : 4 * quad + 4, :].bitcast(I32))
         v_hi = sb.tile([P, T], F32, name="v_hi", tag="v_hi", align_bytes=64)
@@ -94,7 +94,7 @@ def tile_attend_qpk_topk_kernel(tc, q_words, q_scales, k_words, k_scales, vT, vs
         nc.vector.tensor_copy(v_g[0][:], v_lo[:].indirect(offsets[:]))
 
         v_in = lap.tile([P, DV, PACK], BF16, name="v_in", offset=64, align_bytes=64)
-        v_turn = [ps.tile([P, 2, P], F32, name=f"v_turn{h}", tag=("acc1", "vs_turn")[h]) for h in range(2)]
+        v_turn = [ps.tile([P, 2, P], F32, name=f"v_turn{h}", tag=("acc1", "acc0")[h]) for h in range(2)]
         p_turn = [ps.tile([P, PACK, P], F32, name=f"p_turn{i}") for i in range(2)]
 
         def turn_values(h):
@@ -109,8 +109,8 @@ def tile_attend_qpk_topk_kernel(tc, q_words, q_scales, k_words, k_scales, vT, vs
                 nc.tensor.transpose(p_turn[i][:, t, :], prob[i][:, t, :], ident[:])
 
         turn_weights(0)
-        turn_weights(1)
         turn_values(1)
+        turn_weights(1)
         turn_values(0)
 
         w_in = [sb.tile([P, P, PACK], BF16, name=f"w_in{i}", align_bytes=64) for i in range(2)]
@@ -118,7 +118,7 @@ def tile_attend_qpk_topk_kernel(tc, q_words, q_scales, k_words, k_scales, vT, vs
         w_plane = [sb.tile([P, P], U8, name=f"w_plane{i}", align_bytes=64) for i in range(2)]
         v_codes = sb.tile([P, DV], U32, name="v_codes", align_bytes=64)
         v_plane = sb.tile([P, DV], U8, name="v_plane", align_bytes=64)
-        inv = lap.tile([P, 2], F32, name="inv", offset=0, align_bytes=64)
+        inv = sb.tile([P, 2], F32, name="inv")
 
         def weigh(i):
             nc.vector.tensor_tensor(w_in[i][:], p_turn[i][:].rearrange("p t q -> p q t"),
@@ -128,21 +128,22 @@ def tile_attend_qpk_topk_kernel(tc, q_words, q_scales, k_words, k_scales, vT, vs
             nc.vector.quantize_mx(out=w_codes[i][:].bitcast(FP8X4), scales=w_plane[i][:],
                                   in_=w_in[i][:].rearrange("p q t -> p (q t)"))
 
+        nc.vector.reciprocal(inv[:], total[:])
         weigh(0)
         weigh(1)
         quantise_w(0)
         nc.vector.quantize_mx(out=v_codes[:].bitcast(FP8X4), scales=v_plane[:], in_=v_in[:].rearrange("p e t -> p (e t)"))
         quantise_w(1)
-        nc.vector.reciprocal(inv[:], total[:])
 
         for i in range(2):
-            y = ps.tile([P, DV], F32, name=f"y{i}", tag=("acc0", "y1")[i])
-            nc.tensor.matmul_mx(out=y[:], lhsT=w_codes[i][:].bitcast(FP8X4), lhsT_scale=w_plane[i][:],
-                                rhs=v_codes[:].bitcast(FP8X4), rhs_scale=v_plane[:], start=True, stop=True)
             res = sb.tile([P, DV], F32, name=f"res{i}", align_bytes=64)
-            if i == 0:
-                nc.scalar.activation(res[:], y[:], ACT.Copy, scale=inv[:, i : i + 1])
-                nc.scalar.dma_start(out[0, i * P : (i + 1) * P, :], res[:])
-            else:
-                nc.vector.tensor_scalar(res[:], y[:], inv[:, i : i + 1], None, ALU.mult)
-                nc.sync.dma_start(out[0, i * P : (i + 1) * P, :], res[:])
+            for h in range(2):
+                cols = slice(h * P, (h + 1) * P)
+                y = ps.tile([P, P], F32, name=f"y{i}{h}", tag=("vs_turn", "y01", "y10", "y11")[2 * i + h])
+                nc.tensor.matmul_mx(out=y[:], lhsT=w_codes[i][:].bitcast(FP8X4), lhsT_scale=w_plane[i][:],
+                                    rhs=v_codes[:, cols].bitcast(FP8X4), rhs_scale=v_plane[:, cols], start=True, stop=True)
+                if h == 0:
+                    nc.vector.tensor_scalar(res[:, cols], y[:], inv[:, i : i + 1], None, ALU.mult)
+                else:
+                    nc.scalar.activation(res[:, cols], y[:], ACT.Copy, scale=inv[:, i : i + 1])
+            nc.sync.dma_start(out[0, i * P : (i + 1) * P, :], res[:])

from contextlib import ExitStack

import concourse.mybir as mybir
from concourse.masks import make_identity

F32 = mybir.dt.float32
BF16 = mybir.dt.bfloat16
I32 = mybir.dt.int32
U32 = mybir.dt.uint32
U16 = mybir.dt.uint16
U8 = mybir.dt.uint8
FP8X4 = mybir.dt.float8_e4m3fn_x4
ACT = mybir.ActivationFunctionType
ALU = mybir.AluOpType
AXIS = mybir.AxisListType

P = 128
PACK = 4
N, T, D, DV, NQ = 512, 1024, 512, 256, 256
FLOPS = 2 * NQ * N * D + 2 * NQ * N * DV
BYTES = 4 * P * NQ + 16 * NQ + 4 * P * T + 16 * T + 4 * DV * T + 4 * T + 2 * P * (N // 16) + 4 * NQ * DV


def tile_attend_qpk_topk_kernel(tc, q_words, q_scales, k_words, k_scales, vT, vs, offs, out):
    nc = tc.nc
    with ExitStack() as ctx:
        sb = ctx.enter_context(tc.tile_pool(name="sb", bufs=1))
        lap = ctx.enter_context(tc.tile_pool(name="lap", bufs=1))
        ps = ctx.enter_context(tc.psum_pool(name="ps", bufs=1))

        offsets = sb.tile([P, N // 16], U16, name="offsets")
        k_pool = sb.tile([P, T], U32, name="k_pool", tag="late", align_bytes=64)
        ks_pool = sb.tile([P, T], U8, name="ks_pool", align_bytes=64)
        vs_pool = lap.tile([P, T], F32, name="vs_pool", offset=0, align_bytes=64)
        q_plane = sb.tile([P, NQ], U8, name="q_plane", align_bytes=64)
        ident = sb.tile([P, P], F32, name="ident", align_bytes=64)
        warm_in = sb.tile([P, 1], F32, name="warm_in", tag="v_hi", align_bytes=64)
        warm_out = sb.tile([P, 1], F32, name="warm_out", tag="q_codes", align_bytes=64)

        nc.vector.memset(ks_pool[:].bitcast(I32), 0)
        nc.vector.memset(warm_in[:], 0.0)
        nc.vector.memset(vs_pool[:, : T - P].bitcast(I32), 0)
        nc.vector.memset(q_plane[:].bitcast(I32), 0)
        nc.vector.memset(vs_pool[:, T - P :].bitcast(I32), 0)
        make_identity(nc, ident[:])
        nc.scalar.activation(warm_out[:], warm_in[:], ACT.Exp)

        nc.sync.dma_start(k_pool[:].bitcast(I32), k_words[0].rearrange("p t r -> p (t r)").bitcast(I32))
        nc.sync.dma_start(offsets[:], offs)
        for quad in range(4):
            nc.sync.dma_start(ks_pool[32 * quad : 32 * quad + 4, :].bitcast(I32), k_scales[0, 4 * quad : 4 * quad + 4, :].bitcast(I32))
        v_hi = sb.tile([P, T], F32, name="v_hi", tag="v_hi", align_bytes=64)
        q_codes = sb.tile([P, NQ], U32, name="q_codes", tag="q_codes", align_bytes=64)
        nc.sync.dma_start(v_hi[:], vT[P : 2 * P, :])
        nc.sync.dma_start(q_codes[:].bitcast(I32), q_words[0, 0].rearrange("p t r -> p (t r)").bitcast(I32))
        for quad in range(4):
            nc.sync.dma_start(q_plane[32 * quad : 32 * quad + 4, :].bitcast(I32), q_scales[0, 0, 4 * quad : 4 * quad + 4, :].bitcast(I32))
        nc.sync.dma_start(vs_pool[0:1, :], vs[0:1, :])

        ks_g = sb.tile([P, N], U8, name="ks_g", align_bytes=64)
        k_g = lap.tile([P, N], U32, name="k_g", offset=4096, align_bytes=64)
        vs_g = sb.tile([P, N], F32, name="vs_g", align_bytes=64)
        nc.vector.tensor_copy(k_g[:], k_pool[:].indirect(offsets[:]))
        nc.vector.tensor_copy(ks_g[:], ks_pool[:].indirect(offsets[:]))
        v_lo = sb.tile([P, T], F32, name="v_lo", tag="late", align_bytes=64)
        nc.sync.dma_start(v_lo[:], vT[0:P, :])

        score = [ps.tile([P, N], F32, name=f"score{i}", tag=f"acc{i}") for i in range(2)]
        for i in range(2):
            cols = slice(i * P, (i + 1) * P)
            nc.tensor.matmul_mx(out=score[i][:], lhsT=q_codes[:, cols].bitcast(FP8X4), lhsT_scale=q_plane[:, cols],
                                rhs=k_g[:].bitcast(FP8X4), rhs_scale=ks_g[:], start=True, stop=True)

        nc.vector.tensor_copy(vs_g[:], vs_pool[:].indirect(offsets[:]))
        vs_turn = ps.tile([P, PACK, P], F32, name="vs_turn", tag="vs_turn")
        for t in range(PACK):
            nc.tensor.transpose(vs_turn[:, t, :], vs_g[:, t:N:PACK], ident[:])

        v_g = [lap.tile([P, N], BF16, name=f"v_g{h}", offset=(3584, 6144)[h], align_bytes=64) for h in range(2)]
        v_bf = sb.tile([P, T], BF16, name="v_bf", align_bytes=64)
        nc.scalar.copy(v_bf[:], v_hi[:])
        nc.scalar.activation(v_g[1][:], v_bf[:].indirect(offsets[:]), ACT.Copy)

        neg_max = [lap.tile([P, 1], F32, name=f"neg_max{i}", offset=64 * i, align_bytes=64) for i in range(2)]
        total = sb.tile([P, 2], F32, name="total")
        prob = [sb.tile([P, PACK, P], F32, name=f"prob{i}", align_bytes=64) for i in range(2)]
        for i in range(2):
            nc.vector.tensor_reduce(neg_max[i][:], score[i][:], AXIS.X, ALU.max, negate=True)
        for i in range(2):
            nc.scalar.activation(prob[i][:], score[i][:].rearrange("p (s t) -> p t s", t=PACK), ACT.Exp,
                                 bias=neg_max[i][:], scale=1.0, accum_out=total[:, i : i + 1])
        vs_col = lap.tile([P, 1, PACK], F32, name="vs_col", offset=0, align_bytes=64)
        nc.scalar.copy(vs_col[:, 0, :], vs_turn[:, :, 0])
        nc.vector.tensor_copy(v_g[0][:], v_lo[:].indirect(offsets[:]))

        v_in = lap.tile([P, DV, PACK], BF16, name="v_in", offset=64, align_bytes=64)
        v_turn = [ps.tile([P, 2, P], F32, name=f"v_turn{h}", tag=("acc1", "acc0")[h]) for h in range(2)]
        p_turn = [ps.tile([P, PACK, P], F32, name=f"p_turn{i}") for i in range(2)]

        def turn_values(h):
            words = v_g[h][:].bitcast(F32)
            for u in range(2):
                nc.tensor.transpose(v_turn[h][:, u, :], words[:, u : N // 2 : 2], ident[:])
            dst = v_in[:, h * P : (h + 1) * P, :].rearrange("p e t -> p (e t)").bitcast(F32)
            nc.scalar.copy(dst.rearrange("p (e u) -> p e u", u=2), v_turn[h][:].rearrange("p u e -> p e u"))

        def turn_weights(i):
            for t in range(PACK):
                nc.tensor.transpose(p_turn[i][:, t, :], prob[i][:, t, :], ident[:])

        turn_weights(0)
        turn_values(1)
        turn_weights(1)
        turn_values(0)

        w_in = [sb.tile([P, P, PACK], BF16, name=f"w_in{i}", align_bytes=64) for i in range(2)]
        w_codes = [sb.tile([P, P], U32, name=f"w_codes{i}", align_bytes=64) for i in range(2)]
        w_plane = [sb.tile([P, P], U8, name=f"w_plane{i}", align_bytes=64) for i in range(2)]
        v_codes = sb.tile([P, DV], U32, name="v_codes", align_bytes=64)
        v_plane = sb.tile([P, DV], U8, name="v_plane", align_bytes=64)
        inv = sb.tile([P, 2], F32, name="inv")

        def weigh(i):
            nc.vector.tensor_tensor(w_in[i][:], p_turn[i][:].rearrange("p t q -> p q t"),
                                    vs_col[:].to_broadcast([P, P, PACK]), ALU.mult)

        def quantise_w(i):
            nc.vector.quantize_mx(out=w_codes[i][:].bitcast(FP8X4), scales=w_plane[i][:],
                                  in_=w_in[i][:].rearrange("p q t -> p (q t)"))

        nc.vector.reciprocal(inv[:], total[:])
        weigh(0)
        weigh(1)
        quantise_w(0)
        nc.vector.quantize_mx(out=v_codes[:].bitcast(FP8X4), scales=v_plane[:], in_=v_in[:].rearrange("p e t -> p (e t)"))
        quantise_w(1)

        for i in range(2):
            res = sb.tile([P, DV], F32, name=f"res{i}", align_bytes=64)
            for h in range(2):
                cols = slice(h * P, (h + 1) * P)
                y = ps.tile([P, P], F32, name=f"y{i}{h}", tag=("vs_turn", "y01", "y10", "y11")[2 * i + h])
                nc.tensor.matmul_mx(out=y[:], lhsT=w_codes[i][:].bitcast(FP8X4), lhsT_scale=w_plane[i][:],
                                    rhs=v_codes[:, cols].bitcast(FP8X4), rhs_scale=v_plane[:, cols], start=True, stop=True)
                if h == 0:
                    nc.vector.tensor_scalar(res[:, cols], y[:], inv[:, i : i + 1], None, ALU.mult)
                else:
                    nc.scalar.activation(res[:, cols], y[:], ACT.Copy, scale=inv[:, i : i + 1])
            nc.sync.dma_start(out[0, i * P : (i + 1) * P, :], res[:])
